import numpy as np
import ml_dtypes


def mxq(x, axis, fmt="e4m3"):
    dtype, down = {"e4m3": (ml_dtypes.float8_e4m3fn, 7), "e5m2": (ml_dtypes.float8_e5m2, 14)}[fmt]
    v = np.moveaxis(np.asarray(x, np.float32).astype(ml_dtypes.bfloat16).astype(np.float64), axis, -1)
    blocks = v.reshape(v.shape[:-1] + (-1, 32))
    amax = np.abs(blocks).max(-1, keepdims=True)
    byte = np.maximum(np.where(amax > 0, np.frexp(amax)[1] - 1 + 127, 0) - down, 1)
    scale = np.exp2(byte - 127.0)
    codes = (blocks / scale).astype(np.float32).astype(dtype).astype(np.float64)
    return np.moveaxis((codes * scale).reshape(v.shape), -1, axis)


WIDE = False


def mx_kscale(k):
    if not WIDE:
        return np.ones(k)
    levels = np.array([10, -10, 5, -5, 0])
    if k % 512:
        return np.exp2(np.random.permutation(np.resize(levels, k // 32))).repeat(32)
    a = np.empty((k // 512, 16))
    for p in range(k // 512):
        a[p, :8] = np.random.permutation(np.resize(levels, 8))
        for g in range(8):
            far = levels[np.abs(levels - a[p, g]) >= 10]
            a[p, g + 8] = far[np.random.randint(len(far))]
    return np.exp2(a.ravel()).repeat(32)


def f64(x):
    return np.asarray(x).astype(np.float64)


def striped(idx):
    return np.tile(idx.reshape(-1, 16).T, (8, 1)).astype(np.uint16)


def unstriped(offs):
    return offs[:16].T.reshape(-1).astype(np.int64)


E2M1 = np.array([0.0, 0.5, 1.0, 1.5, 2.0, 3.0, 4.0, 6.0, -0.0, -0.5, -1.0, -1.5, -2.0, -3.0, -4.0, -6.0])


def pack_weight(w, fmt):
    k, n = w.shape
    w = f64(np.asarray(w, np.float32).astype(ml_dtypes.bfloat16)).reshape(k // 32, 32, n)
    amax = np.abs(w).max(1)
    if fmt == "e4m3":
        byte = np.frexp(amax)[1] - 1 + 127 - 7
    else:
        mant, ex = np.frexp(amax / 6.0)
        byte = np.where(mant > 0.5, ex, ex - 1) + 127
    byte = np.clip(np.where(amax > 0, byte, 1), 1, 254)
    scaled = (w * np.exp2(127.0 - byte)[:, None, :]).reshape(k, n).astype(np.float32)
    by_word = np.ascontiguousarray(scaled.reshape(k // 512, 128, 4, n).transpose(0, 1, 3, 2))
    if fmt == "e4m3":
        words = by_word.astype(ml_dtypes.float8_e4m3fn).view(np.uint8)
    else:
        c = by_word.astype(ml_dtypes.float4_e2m1fn).view(np.uint8) & 0xF
        words = (c[..., 0::2] | (c[..., 1::2] << 4)).reshape(k // 512, 128, 2 * n)
    return np.ascontiguousarray(words), np.ascontiguousarray(byte.astype(np.uint8).reshape(k // 512, 16, n))


def unpack_weight(words, scales, fmt):
    g, _, n = scales.shape
    words = np.ascontiguousarray(words).reshape(g, 128, n, -1)
    if fmt == "e4m3":
        vals = words.view(ml_dtypes.float8_e4m3fn).astype(np.float64)
    else:
        nib = np.empty((g, 128, n, 4), np.uint8)
        nib[..., 0::2] = words & 0xF
        nib[..., 1::2] = words >> 4
        vals = E2M1[nib]
    vals = vals * np.repeat(np.exp2(scales.astype(np.float64) - 127.0), 8, axis=1)[..., None]
    return vals.transpose(0, 1, 3, 2).reshape(g * 512, n)


def gelu(v):
    return 0.5 * v * (1.0 + np.tanh(np.sqrt(2.0 / np.pi) * (v + 0.044715 * v**3)))


def bf(x):
    return np.asarray(x, np.float32).astype(ml_dtypes.bfloat16)


def planes(Y):
    n, m = Y.shape
    b = f64(bf(Y)).reshape(n // 32, 32, m)
    amax = np.abs(b).max(1)
    byte = np.clip(np.where(amax > 0, np.frexp(amax)[1] - 1 + 127 - 7, 1), 1, 254)
    codes = (b * np.exp2(127.0 - byte)[:, None, :]).reshape(n, m).astype(np.float32).astype(ml_dtypes.float8_e4m3fn).view(np.uint8)
    words = codes.reshape(n // 512, 128, 4, m).transpose(0, 1, 3, 2)
    return np.ascontiguousarray(words), np.ascontiguousarray(byte.astype(np.uint8).reshape(n // 512, 16, m))


K, T, H, N, S, P = 512, 4096, 1024, 512, 1024, 512


def setup_inputs():
    n = np.random.standard_normal
    s = mx_kscale(K)[:, None]
    u = mx_kscale(H)[:, None]
    tab_words, tab_scales = pack_weight(n((K, T)) * s, "e4m3")
    w2_words, w2_scales = pack_weight(n((K, H)) / np.sqrt(K) / s * u.T, "e2m1")
    wc_words, wc_scales = pack_weight(n((H, N)) / np.sqrt(H) / u, "e4m3")
    return {
        "tab_words": tab_words, "tab_scales": tab_scales,
        "offs": striped(np.random.permutation(T)[:S]),
        "pos1": striped(np.random.permutation(S)[:P]),
        "pos2": striped(np.random.permutation(S)[:P]),
        "w1": (n((K, H)) / np.sqrt(K) / s * u.T).astype(np.float32),
        "w2_words": w2_words, "w2_scales": w2_scales,
        "wa": (0.65 * n((H, N)) / np.sqrt(H) / u).astype(np.float32),
        "wb": (0.6 * n((K, N)) / np.sqrt(K) / s).astype(np.float32),
        "wc_words": wc_words, "wc_scales": wc_scales,
        "scale": np.random.uniform(0.6, 3.0, N).astype(np.float32),
        "thresh": n(N).astype(np.float32),
        "slot": n((N, P)).astype(np.float32),
        "gain": np.exp(0.8 * n(N)).astype(np.float32),
    }


def reference(tab_words, tab_scales, offs, pos1, pos2, w1, w2_words, w2_scales, wa, wb,
              wc_words, wc_scales, scale, thresh, slot, gain):
    v = unpack_weight(tab_words, tab_scales, "e4m3")[:, unstriped(offs)]
    w2 = unpack_weight(w2_words, w2_scales, "e2m1")
    wc = unpack_weight(wc_words, wc_scales, "e4m3")
    h = np.minimum(mxq(f64(w1), 0, "e4m3").T @ v, w2.T @ v)
    hq = mxq(h, 0, "e4m3")
    e = mxq(f64(wa), 0, "e4m3").T @ hq + mxq(f64(wb), 0, "e4m3").T @ v
    d = wc.T @ hq
    a = 1.0 / (1.0 + np.exp(-(f64(scale)[:, None] * e[:, unstriped(pos1)] + f64(thresh)[:, None])))
    c = d[:, unstriped(pos2)]
    y = (c * f64(slot) + a) * a * f64(gain)[:, None]
    words, scales = planes(y)
    return y, words, scales

@@ -1,0 +1,288 @@
+from contextlib import ExitStack
+
+import concourse.mybir as mybir
+
+K, T, H, N, S, M = 512, 4096, 1024, 512, 1024, 512
+FLOPS = 2 * (2 * K * H * S + H * N * S + K * N * S + H * N * S)
+
+F32 = mybir.dt.float32
+BF16 = mybir.dt.bfloat16
+I32 = mybir.dt.int32
+U32 = mybir.dt.uint32
+U16 = mybir.dt.uint16
+U8 = mybir.dt.uint8
+FP8X4 = mybir.dt.float8_e4m3fn_x4
+FP4X4 = mybir.dt.float4_e2m1fn_x4
+ALU = mybir.AluOpType
+ACT = mybir.ActivationFunctionType
+
+P = 128
+PACK = 4
+PASS = P * PACK
+BANK = 512
+CHUNK = BANK // PACK
+
+
+def tile_list_ferry_charging_scores_kernel(
+    tc, tab_words, tab_scales, offs, pos1, pos2, w1, w2_words, w2_scales, wa, wb,
+    wc_words, wc_scales, scale, thresh, slot, gain, out_0, out_1, out_2,
+):
+    nc = tc.nc
+    with ExitStack() as ctx:
+        keep = ctx.enter_context(tc.tile_pool(name="keep", bufs=1))
+        reused = ctx.enter_context(tc.tile_pool(name="reused", bufs=1))
+        ring = ctx.enter_context(tc.tile_pool(name="ring", bufs=2))
+        deep = ctx.enter_context(tc.tile_pool(name="deep", bufs=16))
+        psum = ctx.enter_context(tc.psum_pool(name="psum", bufs=1))
+
+        def held(shape, dtype, name, tag=None):
+            return keep.tile(shape, dtype, name=name, tag=tag or name, align_bytes=64)
+
+        tab_scale_rows = held([P, T], U8, "tab_scale_rows")
+        w2_scale_rows = held([P, H], U8, "w2_scale_rows")
+        nc.vector.memset(tab_scale_rows[:].bitcast(I32), 0)
+        nc.gpsimd.memset(w2_scale_rows[:].bitcast(I32), 0)
+
+        offs_t = keep.tile([P, S // 16], U16, name="offs_t")
+        pos1_t = keep.tile([P, M // 16], U16, name="pos1_t")
+        pos2_t = keep.tile([P, M // 16], U16, name="pos2_t")
+        nc.sync.dma_start(offs_t[:], offs)
+        nc.sync.dma_start(pos1_t[:], pos1)
+        nc.sync.dma_start(pos2_t[:], pos2)
+        w2_raw = held([P, H], U16, "w2_raw")
+        nc.sync.dma_start(w2_raw[:].bitcast(I32), w2_words[0].bitcast(I32))
+        tab = reused.tile([P, T], I32, name="tab", offset=0, align_bytes=64)
+        nc.sync.dma_start(tab[:], tab_words[0].rearrange("p t i -> p (t i)").bitcast(I32))
+        for q in range(4):
+            nc.scalar.dma_start(
+                tab_scale_rows[32 * q : 32 * q + 4, :].bitcast(I32), tab_scales[0, 4 * q : 4 * q + 4, :].bitcast(I32)
+            )
+        for q in range(4):
+            queue = nc.gpsimd if q < 2 else nc.scalar
+            queue.dma_start(
+                w2_scale_rows[32 * q : 32 * q + 4, :].bitcast(I32), w2_scales[0, 4 * q : 4 * q + 4, :].bitcast(I32)
+            )
+
+        def load_rows(raw, rows):
+            nc.sync.dma_start(raw, rows.rearrange("(p j) c -> p j c", j=PACK))
+            return raw
+
+        def round_weight(engine, raw):
+            rounded = ring.tile([P, PACK * N], BF16, name="rounded", align_bytes=64)
+            out = rounded[:].rearrange("p (t m j) -> p m j t", t=PACK, j=PACK)
+            src = raw.rearrange("p j (m t) -> p m j t", t=PACK)
+            if engine == "scalar":
+                nc.scalar.copy(out=out, in_=src)
+            else:
+                nc.vector.tensor_copy(out=out, in_=src)
+            return rounded
+
+        def quantize(rounded, name):
+            width = rounded.shape[1] // PACK
+            codes = held([P, width], U32, name + "_codes")
+            scales = held([P, width], U8, name + "_scales")
+            nc.vector.quantize_mx(out=codes[:].bitcast(FP8X4), scales=scales[:], in_=rounded[:])
+            return codes, scales
+
+        def mm(out, lhs, lhs_cols, rhs, rhs_cols, start, stop, lhs_dtype=FP8X4, lhs_row=0):
+            nc.tensor.matmul_mx(
+                out=out,
+                lhsT=lhs[0][:, lhs_cols].bitcast(lhs_dtype), lhsT_scale=lhs[1][lhs_row:P, lhs_cols],
+                rhs=rhs[0][:, rhs_cols].bitcast(FP8X4), rhs_scale=rhs[1][:, rhs_cols],
+                start=start, stop=stop,
+            )
+
+        w2_codes = held([P, H], U16, "w2_codes")
+        w2_plane = held([P, H], U8, "w2_plane")
+        nc.vector.tensor_copy(
+            out=w2_codes[:].rearrange("p (b t m) -> p b t m", b=2, t=PACK),
+            in_=w2_raw[:].rearrange("p (b m t) -> p b t m", b=2, t=PACK),
+        )
+        early = held([P, 3, PACK, N], F32, "early", tag="w2_raw")
+        w1_raw = [load_rows(early[:, b], w1[:, b * PASS : (b + 1) * PASS]) for b in range(2)]
+        wb_raw = load_rows(early[:, 2], wb)
+        v_plane = held([P, S], U8, "v_plane")
+        nc.vector.tensor_copy(out=v_plane[:], in_=tab_scale_rows[:].indirect(offs_t[:]))
+        v_codes = held([P, S], U32, "v_codes", tag="tab_scale_rows")
+        nc.vector.tensor_copy(
+            out=w2_plane[:].rearrange("p (b t m) -> p b t m", b=2, t=PACK),
+            in_=w2_scale_rows[:].rearrange("p (b m t) -> p b t m", b=2, t=PACK),
+        )
+        for lo, hi in ((0, 256), (256, 512), (512, 1024)):
+            nc.vector.tensor_copy(
+                out=v_codes[:, lo:hi], in_=tab[:].bitcast(U32).indirect(offs_t[:, lo // 16 : hi // 16])
+            )
+        wa_tile0 = reused.tile([P, PACK, N], F32, name="wa_tile0", offset=0, align_bytes=64)
+        wc_raw = reused.tile([P, 2, N], I32, name="wc_raw", offset=8192, align_bytes=64)
+        wa_tile1 = reused.tile([P, PACK, N], F32, name="wa_tile1", offset=12288, align_bytes=64)
+        wa_raw0 = load_rows(wa_tile0[:], wa[0:PASS, :])
+        nc.sync.dma_start(wc_raw[:], wc_words.rearrange("a p c i -> p a (c i)").bitcast(I32))
+        wa_raw1 = load_rows(wa_tile1[:], wa[PASS : 2 * PASS, :])
+        wc_scale_rows = held([P, N], U8, "wc_scale_rows", tag="w2_scale_rows")
+        nc.vector.memset(wc_scale_rows[:].bitcast(I32), 0)
+        for q in range(4):
+            nc.sync.dma_start(
+                wc_scale_rows[32 * q : 32 * q + 8, :].bitcast(I32), wc_scales[:, 4 * q : 4 * q + 4, :].bitcast(I32)
+            )
+        v = (v_codes, v_plane)
+        w2 = (w2_codes, w2_plane)
+
+        def second_reading(b, c):
+            bank = psum.tile([P, PACK, CHUNK], F32, name="bank2", bufs=3)
+            for t in range(PACK):
+                lo = b * PASS + t * P
+                mm(bank[:, t, :], w2, slice(lo, lo + P), v, slice(c * CHUNK, (c + 1) * CHUNK), True, True, FP4X4)
+            h2 = deep.tile([P, CHUNK, PACK], F32, name="h2")
+            nc.scalar.copy(out=h2[:], in_=bank[:].rearrange("p t n -> p n t"))
+            return h2
+
+        def first_reading(w1q, c, h2, h_rounded):
+            bank = psum.tile([P, PACK, CHUNK], F32, name="bank1", bufs=2)
+            for t in range(PACK):
+                mm(bank[:, t, :], w1q, slice(t * P, (t + 1) * P), v, slice(c * CHUNK, (c + 1) * CHUNK), True, True)
+            lo = (c % PACK) * BANK
+            nc.vector.tensor_tensor(
+                out=h_rounded[:, lo : lo + BANK].rearrange("p (n t) -> p n t", t=PACK),
+                in0=bank[:].rearrange("p t n -> p n t"), in1=h2[:], op=ALU.min,
+            )
+
+        e_rows = [held([P, S], F32, "e_rows%d" % t) for t in range(PACK)]
+        d_rows = [held([P, S], F32, "d_rows%d" % t) for t in range(PACK)]
+        whole = slice(0, BANK)
+        hq, h2, waq = {}, {}, {}
+
+        def empty(engine, out, bank):
+            if engine == "scalar":
+                nc.scalar.copy(out=out, in_=bank[:])
+            else:
+                nc.vector.tensor_copy(out=out, in_=bank[:])
+
+        def score_bank(tag):
+            return psum.tile([P, BANK], F32, name=tag, bufs=2 if tag == "bank1" else 3)
+
+        def e_scores(t, half, tag):
+            rows = slice(t * P, (t + 1) * P)
+            cols = slice(half * BANK, (half + 1) * BANK)
+            bank = score_bank(tag)
+            mm(bank[:], wbq, rows, v, cols, True, False)
+            for a in range(2):
+                mm(bank[:], waq[a], rows, hq[a, half], whole, False, a == 1)
+            empty("scalar", e_rows[t][:, cols], bank)
+
+        def d_scores(t, half, tag, engine):
+            rows = slice(t * P, (t + 1) * P)
+            cols = slice(half * BANK, (half + 1) * BANK)
+            bank = score_bank(tag)
+            for a in range(2):
+                mm(bank[:], (wc_codes[:, a, :], wc_plane), rows, hq[a, half], whole, a == 0, a == 1, lhs_row=4 * a)
+            empty(engine, d_rows[t][:, cols], bank)
+
+        def seconds(b, chunks):
+            for c in chunks:
+                h2[b, c] = second_reading(b, c)
+
+        def firsts(b, half, w1q):
+            h_rounded = ring.tile([P, PACK * BANK], BF16, name="h_rounded", align_bytes=64)
+            for c in range(PACK * half, PACK * (half + 1)):
+                first_reading(w1q, c, h2[b, c], h_rounded)
+            return h_rounded
+
+        seconds(0, range(0, 4))
+        w1q0 = quantize(round_weight("vector", w1_raw[0]), "w1q0")
+        w1r1 = round_weight("scalar", w1_raw[1])
+        seconds(0, range(4, 8))
+        r00 = firsts(0, 0, w1q0)
+        w1q1 = quantize(w1r1, "w1q1")
+        seconds(1, range(0, 4))
+        r01 = firsts(0, 1, w1q0)
+        hq[0, 0] = quantize(r00, "hq00")
+        wbr = round_weight("scalar", wb_raw)
+        slot_tile = held([P, PACK, M], F32, "slot_tile", tag="w2_raw")
+        slot_t = load_rows(slot_tile[:], slot)
+        seconds(1, range(4, 8))
+        r10 = firsts(1, 0, w1q1)
+        war0 = round_weight("scalar", wa_raw0)
+        wc_codes = held([P, 2, N], I32, "wc_codes")
+        wc_plane = held([P, N], U8, "wc_plane")
+        nc.vector.tensor_copy(
+            out=wc_codes[:].rearrange("p a (t m) -> p a m t", t=PACK),
+            in_=wc_raw[:].rearrange("p a (m t) -> p a m t", t=PACK),
+        )
+        hq[1, 0] = quantize(r10, "hq10")
+        nc.vector.tensor_copy(
+            out=wc_plane[:].rearrange("p (t m) -> p t m", t=PACK),
+            in_=wc_scale_rows[:].rearrange("p (m t) -> p t m", t=PACK),
+        )
+        row_values = held([P, 3, 8], F32, "row_values", tag="w2_scale_rows")
+        for k, vec in enumerate((scale, thresh, gain)):
+            nc.sync.dma_start(row_values[:, k, 0:PACK], vec.rearrange("(p t) -> p t", t=PACK))
+        row_scale, row_thresh, row_gain = (row_values[:, k, :] for k in range(3))
+        wbq = quantize(wbr, "wbq")
+        for t in range(PACK):
+            d_scores(t, 0, "score", "scalar")
+        war1 = round_weight("vector", wa_raw1)
+        hq[0, 1] = quantize(r01, "hq01")
+        waq[1] = quantize(war1, "waq1")
+        waq[0] = quantize(war0, "waq0")
+        for t in range(PACK):
+            e_scores(t, 0, "score")
+        r11 = firsts(1, 1, w1q1)
+        hq[1, 1] = quantize(r11, "hq11")
+
+
+        HALF = M // 2
+        y = held([P, 2, PACK, HALF], F32, "y")
+        y_rounded = held([P, PACK * M], BF16, "y_rounded")
+        y_codes = held([P, M], I32, "y_codes")
+        y_plane = held([P, M], U8, "y_plane")
+        out_rows = out_0.rearrange("(p t) (h m) -> p h t m", t=PACK, h=2)
+
+        def finish(t, lo, hi):
+            width = hi - lo
+            halves = slice(lo // HALF, hi // HALF)
+            gate = ring.tile([P, width], F32, name="gate")
+            nc.scalar.activation(
+                out=gate[:], in_=e_rows[t][:].indirect(pos1_t[:, lo // 16 : hi // 16]), func=ACT.Sigmoid,
+                bias=row_thresh[:, t : t + 1], scale=row_scale[:, t : t + 1],
+            )
+            weighted = ring.tile([P, width], F32, name="weighted")
+            nc.vector.tensor_tensor(
+                out=weighted[:], in0=d_rows[t][:].indirect(pos2_t[:, lo // 16 : hi // 16]), in1=slot_t[:, t, lo:hi],
+                op=ALU.mult,
+            )
+            total = ring.tile([P, width], F32, name="total")
+            nc.vector.tensor_tensor(out=total[:], in0=weighted[:], in1=gate[:], op=ALU.add)
+            nc.vector.scalar_tensor_tensor(
+                out=y[:, halves, t, :], in0=total[:].rearrange("p (h m) -> p h m", m=HALF),
+                scalar=row_gain[:, t : t + 1], in1=gate[:].rearrange("p (h m) -> p h m", m=HALF),
+                op0=ALU.mult, op1=ALU.mult,
+            )
+            nc.sync.dma_start(out_rows[:, halves, t, :], y[:, halves, t, :])
+
+        def planes(engine, h):
+            cols = slice(h * HALF, (h + 1) * HALF)
+            rounded = y_rounded[:, h * HALF * PACK : (h + 1) * HALF * PACK]
+            out = rounded.rearrange("p (c i t) -> p c t i", i=PACK, t=PACK)
+            src = y[:, h, :, :].rearrange("p t (c i) -> p c t i", i=PACK)
+            if engine == "scalar":
+                nc.scalar.copy(out=out, in_=src)
+            else:
+                nc.vector.tensor_copy(out=out, in_=src)
+            nc.vector.quantize_mx(out=y_codes[:, cols].bitcast(FP8X4), scales=y_plane[:, cols], in_=rounded)
+            nc.sync.dma_start(out_1[0].rearrange("p m t -> p (m t)").bitcast(I32)[:, cols], y_codes[:, cols])
+
+        for t in range(PACK):
+            e_scores(t, 1, "bank2")
+            d_scores(t, 1, "bank1", "vector" if t == 0 else "scalar")
+
+            if t < PACK - 1:
+                finish(t, 0, M)
+        finish(PACK - 1, 0, HALF)
+        finish(PACK - 1, HALF, M)
+        planes("scalar", 0)
+        planes("vector", 1)
+        for q in range(4):
+            queue = nc.scalar if q % 2 else nc.sync
+            queue.dma_start(
+                out_2[0, 4 * q : 4 * q + 4, :].bitcast(I32), y_plane[32 * q : 32 * q + 4, :].bitcast(I32)
+            )

@@ -39,9 +39,7 @@ def tile_list_ferry_charging_scores_kernel(
             return keep.tile(shape, dtype, name=name, tag=tag or name, align_bytes=64)
 
         tab_scale_rows = held([P, T], U8, "tab_scale_rows")
-        w2_scale_rows = held([P, H], U8, "w2_scale_rows")
         nc.vector.memset(tab_scale_rows[:].bitcast(I32), 0)
-        nc.gpsimd.memset(w2_scale_rows[:].bitcast(I32), 0)
 
         offs_t = keep.tile([P, S // 16], U16, name="offs_t")
         pos1_t = keep.tile([P, M // 16], U16, name="pos1_t")
@@ -49,30 +47,38 @@ def tile_list_ferry_charging_scores_kernel(
         nc.sync.dma_start(offs_t[:], offs)
         nc.sync.dma_start(pos1_t[:], pos1)
         nc.sync.dma_start(pos2_t[:], pos2)
-        w2_raw = held([P, H], U16, "w2_raw")
+        w2_raw = reused.tile([P, H], U16, name="w2_raw", offset=0, align_bytes=64)
         nc.sync.dma_start(w2_raw[:].bitcast(I32), w2_words[0].bitcast(I32))
-        tab = reused.tile([P, T], I32, name="tab", offset=0, align_bytes=64)
-        nc.sync.dma_start(tab[:], tab_words[0].rearrange("p t i -> p (t i)").bitcast(I32))
-        for q in range(4):
-            nc.scalar.dma_start(
-                tab_scale_rows[32 * q : 32 * q + 4, :].bitcast(I32), tab_scales[0, 4 * q : 4 * q + 4, :].bitcast(I32)
-            )
-        for q in range(4):
-            queue = nc.gpsimd if q < 2 else nc.scalar
-            queue.dma_start(
-                w2_scale_rows[32 * q : 32 * q + 4, :].bitcast(I32), w2_scales[0, 4 * q : 4 * q + 4, :].bitcast(I32)
-            )
 
         def load_rows(raw, rows):
             nc.sync.dma_start(raw, rows.rearrange("(p j) c -> p j c", j=PACK))
             return raw
 
+        w1_first = held([P, PACK, N], F32, "w1_first")
+        w1_raw0 = load_rows(w1_first[:], w1[:, 0:PASS])
+        wc_raw = held([P, 2, N], I32, "wc_raw")
+        nc.sync.dma_start(wc_raw[:], wc_words.rearrange("a p c i -> p a (c i)").bitcast(I32))
+        for q in range(4):
+            nc.sync.dma_start(
+                tab_scale_rows[32 * q : 32 * q + 4, :].bitcast(I32), tab_scales[0, 4 * q : 4 * q + 4, :].bitcast(I32)
+            )
+
         def round_weight(engine, raw):
-            rounded = ring.tile([P, PACK * N], BF16, name="rounded", align_bytes=64)
+            rounded = ring.tile([P, PACK * N], BF16, name="rounded", align_bytes=64, bufs=3)
             out = rounded[:].rearrange("p (t m j) -> p m j t", t=PACK, j=PACK)
             src = raw.rearrange("p j (m t) -> p m j t", t=PACK)
             if engine == "scalar":
-                nc.scalar.copy(out=out, in_=src)
+                for lo in range(0, P, P // 2):
+                    nc.scalar.copy(out=out[:, lo : lo + P // 2], in_=src[:, lo : lo + P // 2])
+            elif engine == "both":
+                nc.scalar.copy(out=out[:, 0 : P // 2], in_=src[:, 0 : P // 2])
+                nc.vector.tensor_copy(out=out[:, P // 2 : P], in_=src[:, P // 2 : P])
+            elif engine == "gpsimd":
+                for lo in range(0, P, P // 4):
+                    nc.gpsimd.tensor_scalar(
+                        out=out[:, lo : lo + P // 4], in0=src[:, lo : lo + P // 4], scalar1=1.0, scalar2=0.0,
+                        op0=ALU.mult, op1=ALU.add,
+                    )
             else:
                 nc.vector.tensor_copy(out=out, in_=src)
             return rounded
@@ -98,58 +104,75 @@ def tile_list_ferry_charging_scores_kernel(
             out=w2_codes[:].rearrange("p (b t m) -> p b t m", b=2, t=PACK),
             in_=w2_raw[:].rearrange("p (b m t) -> p b t m", b=2, t=PACK),
         )
-        early = held([P, 3, PACK, N], F32, "early", tag="w2_raw")
-        w1_raw = [load_rows(early[:, b], w1[:, b * PASS : (b + 1) * PASS]) for b in range(2)]
-        wb_raw = load_rows(early[:, 2], wb)
+        tab = reused.tile([P, T], I32, name="tab", offset=H, align_bytes=64)
+        nc.sync.dma_start(tab[:], tab_words[0].rearrange("p t i -> p (t i)").bitcast(I32))
+        w2_scale_rows = reused.tile([P, H], U8, name="w2_scale_rows", offset=0, align_bytes=64)
+        nc.vector.memset(w2_scale_rows[:].bitcast(I32), 0)
+        for q in range(4):
+            nc.sync.dma_start(
+                w2_scale_rows[32 * q : 32 * q + 4, :].bitcast(I32), w2_scales[0, 4 * q : 4 * q + 4, :].bitcast(I32)
+            )
         v_plane = held([P, S], U8, "v_plane")
         nc.vector.tensor_copy(out=v_plane[:], in_=tab_scale_rows[:].indirect(offs_t[:]))
-        v_codes = held([P, S], U32, "v_codes", tag="tab_scale_rows")
+        w1r0 = round_weight("scalar", w1_raw0)
+        early = held([P, 2, PACK, N], F32, "early", tag="w1_first")
+        w1_raw1 = load_rows(early[:, 0], w1[:, PASS : 2 * PASS])
+        wb_raw = load_rows(early[:, 1], wb)
+        late = held([P, 2, PACK, N], F32, "late", tag="tab_scale_rows")
+        wa_raw0 = load_rows(late[:, 0], wa[0:PASS, :])
+        wa_raw1 = load_rows(late[:, 1], wa[PASS : 2 * PASS, :])
+        w1q0 = quantize(w1r0, "w1q0")
+        wc_codes = held([P, 2, N], I32, "wc_codes")
         nc.vector.tensor_copy(
-            out=w2_plane[:].rearrange("p (b t m) -> p b t m", b=2, t=PACK),
-            in_=w2_scale_rows[:].rearrange("p (b m t) -> p b t m", b=2, t=PACK),
+            out=wc_codes[:].rearrange("p a (t m) -> p a m t", t=PACK),
+            in_=wc_raw[:].rearrange("p a (m t) -> p a m t", t=PACK),
         )
+        v_pieces = []
         for lo, hi in ((0, 256), (256, 512), (512, 1024)):
-            nc.vector.tensor_copy(
-                out=v_codes[:, lo:hi], in_=tab[:].bitcast(U32).indirect(offs_t[:, lo // 16 : hi // 16])
-            )
-        wa_tile0 = reused.tile([P, PACK, N], F32, name="wa_tile0", offset=0, align_bytes=64)
-        wc_raw = reused.tile([P, 2, N], I32, name="wc_raw", offset=8192, align_bytes=64)
-        wa_tile1 = reused.tile([P, PACK, N], F32, name="wa_tile1", offset=12288, align_bytes=64)
-        wa_raw0 = load_rows(wa_tile0[:], wa[0:PASS, :])
-        nc.sync.dma_start(wc_raw[:], wc_words.rearrange("a p c i -> p a (c i)").bitcast(I32))
-        wa_raw1 = load_rows(wa_tile1[:], wa[PASS : 2 * PASS, :])
-        wc_scale_rows = held([P, N], U8, "wc_scale_rows", tag="w2_scale_rows")
-        nc.vector.memset(wc_scale_rows[:].bitcast(I32), 0)
+            piece = held([P, hi - lo], U32, "v_codes%d" % lo)
+            nc.vector.tensor_copy(out=piece[:], in_=tab[:].bitcast(U32).indirect(offs_t[:, lo // 16 : hi // 16]))
+            v_pieces.append((lo, hi, piece))
+            if lo == 0:
+                nc.vector.tensor_copy(
+                    out=w2_plane[:].rearrange("p (b t m) -> p b t m", b=2, t=PACK),
+                    in_=w2_scale_rows[:].rearrange("p (b m t) -> p b t m", b=2, t=PACK),
+                )
+
+        def v_cols(lo, hi):
+            first, piece = [(a, x) for a, b, x in v_pieces if a <= lo and hi <= b][0]
+            return piece[:, lo - first : hi - first], v_plane[:, lo:hi]
+
+        wc_scale_rows = reused.tile([P, N], U8, name="wc_scale_rows", offset=0, align_bytes=64)
+        nc.gpsimd.memset(wc_scale_rows[:].bitcast(I32), 0)
         for q in range(4):
             nc.sync.dma_start(
                 wc_scale_rows[32 * q : 32 * q + 8, :].bitcast(I32), wc_scales[:, 4 * q : 4 * q + 4, :].bitcast(I32)
             )
-        v = (v_codes, v_plane)
         w2 = (w2_codes, w2_plane)
 
-        def second_reading(b, c):
+        def w1_reading(w1q, c):
             bank = psum.tile([P, PACK, CHUNK], F32, name="bank2", bufs=3)
             for t in range(PACK):
-                lo = b * PASS + t * P
-                mm(bank[:, t, :], w2, slice(lo, lo + P), v, slice(c * CHUNK, (c + 1) * CHUNK), True, True, FP4X4)
-            h2 = deep.tile([P, CHUNK, PACK], F32, name="h2")
-            nc.scalar.copy(out=h2[:], in_=bank[:].rearrange("p t n -> p n t"))
-            return h2
+                mm(bank[:, t, :], w1q, slice(t * P, (t + 1) * P), v_cols(c * CHUNK, (c + 1) * CHUNK), slice(0, CHUNK), True, True)
+            h1 = deep.tile([P, CHUNK, PACK], F32, name="h1")
+            nc.scalar.copy(out=h1[:], in_=bank[:].rearrange("p t n -> p n t"))
+            return h1
 
-        def first_reading(w1q, c, h2, h_rounded):
+        def lesser(b, c, h1, h_rounded):
             bank = psum.tile([P, PACK, CHUNK], F32, name="bank1", bufs=2)
             for t in range(PACK):
-                mm(bank[:, t, :], w1q, slice(t * P, (t + 1) * P), v, slice(c * CHUNK, (c + 1) * CHUNK), True, True)
+                lo = b * PASS + t * P
+                mm(bank[:, t, :], w2, slice(lo, lo + P), v_cols(c * CHUNK, (c + 1) * CHUNK), slice(0, CHUNK), True, True, FP4X4)
             lo = (c % PACK) * BANK
             nc.vector.tensor_tensor(
                 out=h_rounded[:, lo : lo + BANK].rearrange("p (n t) -> p n t", t=PACK),
-                in0=bank[:].rearrange("p t n -> p n t"), in1=h2[:], op=ALU.min,
+                in0=bank[:].rearrange("p t n -> p n t"), in1=h1[:], op=ALU.min,
             )
 
         e_rows = [held([P, S], F32, "e_rows%d" % t) for t in range(PACK)]
         d_rows = [held([P, S], F32, "d_rows%d" % t) for t in range(PACK)]
         whole = slice(0, BANK)
-        hq, h2, waq = {}, {}, {}
+        hq, waq = {}, {}
 
         def empty(engine, out, bank):
             if engine == "scalar":
@@ -164,7 +187,10 @@ def tile_list_ferry_charging_scores_kernel(
             rows = slice(t * P, (t + 1) * P)
             cols = slice(half * BANK, (half + 1) * BANK)
             bank = score_bank(tag)
-            mm(bank[:], wbq, rows, v, cols, True, False)
+            for lo, hi, piece in v_pieces:
+                if cols.start <= lo < cols.stop:
+                    part = bank[:, lo - cols.start : hi - cols.start]
+                    mm(part, wbq, rows, v_cols(lo, hi), slice(0, hi - lo), lo == cols.start, False)
             for a in range(2):
                 mm(bank[:], waq[a], rows, hq[a, half], whole, False, a == 1)
             empty("scalar", e_rows[t][:, cols], bank)
@@ -177,56 +203,42 @@ def tile_list_ferry_charging_scores_kernel(
                 mm(bank[:], (wc_codes[:, a, :], wc_plane), rows, hq[a, half], whole, a == 0, a == 1, lhs_row=4 * a)
             empty(engine, d_rows[t][:, cols], bank)
 
-        def seconds(b, chunks):
-            for c in chunks:
-                h2[b, c] = second_reading(b, c)
-
-        def firsts(b, half, w1q):
+        def h_half(b, half, w1q):
             h_rounded = ring.tile([P, PACK * BANK], BF16, name="h_rounded", align_bytes=64)
             for c in range(PACK * half, PACK * (half + 1)):
-                first_reading(w1q, c, h2[b, c], h_rounded)
+                lesser(b, c, w1_reading(w1q, c), h_rounded)
             return h_rounded
 
-        seconds(0, range(0, 4))
-        w1q0 = quantize(round_weight("vector", w1_raw[0]), "w1q0")
-        w1r1 = round_weight("scalar", w1_raw[1])
-        seconds(0, range(4, 8))
-        r00 = firsts(0, 0, w1q0)
-        w1q1 = quantize(w1r1, "w1q1")
-        seconds(1, range(0, 4))
-        r01 = firsts(0, 1, w1q0)
-        hq[0, 0] = quantize(r00, "hq00")
-        wbr = round_weight("scalar", wb_raw)
-        slot_tile = held([P, PACK, M], F32, "slot_tile", tag="w2_raw")
-        slot_t = load_rows(slot_tile[:], slot)
-        seconds(1, range(4, 8))
-        r10 = firsts(1, 0, w1q1)
-        war0 = round_weight("scalar", wa_raw0)
-        wc_codes = held([P, 2, N], I32, "wc_codes")
         wc_plane = held([P, N], U8, "wc_plane")
-        nc.vector.tensor_copy(
-            out=wc_codes[:].rearrange("p a (t m) -> p a m t", t=PACK),
-            in_=wc_raw[:].rearrange("p a (m t) -> p a m t", t=PACK),
-        )
+
+        def deal_wc_plane():
+            nc.vector.tensor_copy(
+                out=wc_plane[:].rearrange("p (t m) -> p t m", t=PACK),
+                in_=wc_scale_rows[:].rearrange("p (m t) -> p t m", t=PACK),
+            )
+
+        w1r1 = round_weight("both", w1_raw1)
+        w1q1 = quantize(w1r1, "w1q1")
+        r00 = h_half(0, 0, w1q0)
+        wbr = round_weight("scalar", wb_raw)
+        slot_tile = held([P, PACK, M], F32, "slot_tile", tag="w1_first")
+        slot_t = load_rows(slot_tile[:], slot)
+        r01 = h_half(0, 1, w1q0)
+        war0 = round_weight("scalar", wa_raw0)
+        hq[0, 0] = quantize(r00, "hq00")
+        wbq = quantize(wbr, "wbq")
+        r10 = h_half(1, 0, w1q1)
+        war1 = round_weight("vector", wa_raw1)
         hq[1, 0] = quantize(r10, "hq10")
-        nc.vector.tensor_copy(
-            out=wc_plane[:].rearrange("p (t m) -> p t m", t=PACK),
-            in_=wc_scale_rows[:].rearrange("p (m t) -> p t m", t=PACK),
-        )
-        row_values = held([P, 3, 8], F32, "row_values", tag="w2_scale_rows")
+        deal_wc_plane()
+        row_values = reused.tile([P, 3, 8], F32, name="row_values", offset=0, align_bytes=64)
         for k, vec in enumerate((scale, thresh, gain)):
             nc.sync.dma_start(row_values[:, k, 0:PACK], vec.rearrange("(p t) -> p t", t=PACK))
         row_scale, row_thresh, row_gain = (row_values[:, k, :] for k in range(3))
-        wbq = quantize(wbr, "wbq")
-        for t in range(PACK):
-            d_scores(t, 0, "score", "scalar")
-        war1 = round_weight("vector", wa_raw1)
-        hq[0, 1] = quantize(r01, "hq01")
-        waq[1] = quantize(war1, "waq1")
         waq[0] = quantize(war0, "waq0")
-        for t in range(PACK):
-            e_scores(t, 0, "score")
-        r11 = firsts(1, 1, w1q1)
+        waq[1] = quantize(war1, "waq1")
+        hq[0, 1] = quantize(r01, "hq01")
+        r11 = h_half(1, 1, w1q1)
         hq[1, 1] = quantize(r11, "hq11")
 
 
@@ -272,6 +284,8 @@ def tile_list_ferry_charging_scores_kernel(
             nc.sync.dma_start(out_1[0].rearrange("p m t -> p (m t)").bitcast(I32)[:, cols], y_codes[:, cols])
 
         for t in range(PACK):
+            e_scores(t, 0, "score")
+            d_scores(t, 0, "score", "scalar")
             e_scores(t, 1, "bank2")
             d_scores(t, 1, "bank1", "vector" if t == 0 else "scalar")
 
@@ -281,6 +295,7 @@ def tile_list_ferry_charging_scores_kernel(
         finish(PACK - 1, HALF, M)
         planes("scalar", 0)
         planes("vector", 1)
+
         for q in range(4):
             queue = nc.scalar if q % 2 else nc.sync
             queue.dma_start(

@@ -31,6 +31,7 @@ def tile_list_ferry_charging_scores_kernel(
     with ExitStack() as ctx:
         keep = ctx.enter_context(tc.tile_pool(name="keep", bufs=1))
         reused = ctx.enter_context(tc.tile_pool(name="reused", bufs=1))
+        weights = ctx.enter_context(tc.tile_pool(name="weights", bufs=1))
         ring = ctx.enter_context(tc.tile_pool(name="ring", bufs=2))
         deep = ctx.enter_context(tc.tile_pool(name="deep", bufs=16))
         psum = ctx.enter_context(tc.psum_pool(name="psum", bufs=1))
@@ -41,23 +42,24 @@ def tile_list_ferry_charging_scores_kernel(
         tab_scale_rows = held([P, T], U8, "tab_scale_rows")
         nc.vector.memset(tab_scale_rows[:].bitcast(I32), 0)
 
+        w2_raw = [
+            reused.tile([P, PASS], U16, name="w2_raw%d" % b, offset=b * (H + 4 * T), align_bytes=64) for b in range(2)
+        ]
         offs_t = keep.tile([P, S // 16], U16, name="offs_t")
         pos1_t = keep.tile([P, M // 16], U16, name="pos1_t")
         pos2_t = keep.tile([P, M // 16], U16, name="pos2_t")
+        for b in range(2):
+            nc.sync.dma_start(w2_raw[b][:].bitcast(I32), w2_words[0, :, b * H : (b + 1) * H].bitcast(I32))
         nc.sync.dma_start(offs_t[:], offs)
         nc.sync.dma_start(pos1_t[:], pos1)
         nc.sync.dma_start(pos2_t[:], pos2)
-        w2_raw = reused.tile([P, H], U16, name="w2_raw", offset=0, align_bytes=64)
-        nc.sync.dma_start(w2_raw[:].bitcast(I32), w2_words[0].bitcast(I32))
 
         def load_rows(raw, rows):
             nc.sync.dma_start(raw, rows.rearrange("(p j) c -> p j c", j=PACK))
             return raw
 
-        w1_first = held([P, PACK, N], F32, "w1_first")
+        w1_first = weights.tile([P, PACK, N], F32, name="w1_first", offset=0, align_bytes=64)
         w1_raw0 = load_rows(w1_first[:], w1[:, 0:PASS])
-        wc_raw = held([P, 2, N], I32, "wc_raw")
-        nc.sync.dma_start(wc_raw[:], wc_words.rearrange("a p c i -> p a (c i)").bitcast(I32))
         for q in range(4):
             nc.sync.dma_start(
                 tab_scale_rows[32 * q : 32 * q + 4, :].bitcast(I32), tab_scales[0, 4 * q : 4 * q + 4, :].bitcast(I32)
@@ -83,11 +85,15 @@ def tile_list_ferry_charging_scores_kernel(
                 nc.vector.tensor_copy(out=out, in_=src)
             return rounded
 
-        def quantize(rounded, name):
+        def quantize(rounded, name, cuts=()):
             width = rounded.shape[1] // PACK
             codes = held([P, width], U32, name + "_codes")
             scales = held([P, width], U8, name + "_scales")
-            nc.vector.quantize_mx(out=codes[:].bitcast(FP8X4), scales=scales[:], in_=rounded[:])
+            edges = (0, *cuts, width)
+            for lo, hi in zip(edges, edges[1:]):
+                nc.vector.quantize_mx(
+                    out=codes[:, lo:hi].bitcast(FP8X4), scales=scales[:, lo:hi], in_=rounded[:, PACK * lo : PACK * hi]
+                )
             return codes, scales
 
         def mm(out, lhs, lhs_cols, rhs, rhs_cols, start, stop, lhs_dtype=FP8X4, lhs_row=0):
@@ -100,13 +106,14 @@ def tile_list_ferry_charging_scores_kernel(
 
         w2_codes = held([P, H], U16, "w2_codes")
         w2_plane = held([P, H], U8, "w2_plane")
-        nc.vector.tensor_copy(
-            out=w2_codes[:].rearrange("p (b t m) -> p b t m", b=2, t=PACK),
-            in_=w2_raw[:].rearrange("p (b m t) -> p b t m", b=2, t=PACK),
-        )
-        tab = reused.tile([P, T], I32, name="tab", offset=H, align_bytes=64)
+        for b in range(2):
+            nc.vector.tensor_copy(
+                out=w2_codes[:, b * PASS : (b + 1) * PASS].rearrange("p (t m) -> p t m", t=PACK),
+                in_=w2_raw[b][:].rearrange("p (m t) -> p t m", t=PACK),
+            )
+        tab = reused.tile([P, T], I32, name="tab", offset=0, align_bytes=64)
         nc.sync.dma_start(tab[:], tab_words[0].rearrange("p t i -> p (t i)").bitcast(I32))
-        w2_scale_rows = reused.tile([P, H], U8, name="w2_scale_rows", offset=0, align_bytes=64)
+        w2_scale_rows = reused.tile([P, H], U8, name="w2_scale_rows", offset=H + 4 * T, align_bytes=64)
         nc.vector.memset(w2_scale_rows[:].bitcast(I32), 0)
         for q in range(4):
             nc.sync.dma_start(
@@ -115,18 +122,14 @@ def tile_list_ferry_charging_scores_kernel(
         v_plane = held([P, S], U8, "v_plane")
         nc.vector.tensor_copy(out=v_plane[:], in_=tab_scale_rows[:].indirect(offs_t[:]))
         w1r0 = round_weight("scalar", w1_raw0)
-        early = held([P, 2, PACK, N], F32, "early", tag="w1_first")
+        early = weights.tile([P, 4, PACK, N], F32, name="early", offset=4 * H, align_bytes=64)
         w1_raw1 = load_rows(early[:, 0], w1[:, PASS : 2 * PASS])
+        wc_raw = weights.tile([P, 2, N], I32, name="wc_raw", offset=0, align_bytes=64)
+        nc.sync.dma_start(wc_raw[:], wc_words.rearrange("a p c i -> p a (c i)").bitcast(I32))
         wb_raw = load_rows(early[:, 1], wb)
-        late = held([P, 2, PACK, N], F32, "late", tag="tab_scale_rows")
-        wa_raw0 = load_rows(late[:, 0], wa[0:PASS, :])
-        wa_raw1 = load_rows(late[:, 1], wa[PASS : 2 * PASS, :])
+        wa_raw0 = load_rows(early[:, 2], wa[0:PASS, :])
+        wa_raw1 = load_rows(early[:, 3], wa[PASS : 2 * PASS, :])
         w1q0 = quantize(w1r0, "w1q0")
-        wc_codes = held([P, 2, N], I32, "wc_codes")
-        nc.vector.tensor_copy(
-            out=wc_codes[:].rearrange("p a (t m) -> p a m t", t=PACK),
-            in_=wc_raw[:].rearrange("p a (m t) -> p a m t", t=PACK),
-        )
         v_pieces = []
         for lo, hi in ((0, 256), (256, 512), (512, 1024)):
             piece = held([P, hi - lo], U32, "v_codes%d" % lo)
@@ -142,7 +145,7 @@ def tile_list_ferry_charging_scores_kernel(
             first, piece = [(a, x) for a, b, x in v_pieces if a <= lo and hi <= b][0]
             return piece[:, lo - first : hi - first], v_plane[:, lo:hi]
 
-        wc_scale_rows = reused.tile([P, N], U8, name="wc_scale_rows", offset=0, align_bytes=64)
+        wc_scale_rows = reused.tile([P, N], U8, name="wc_scale_rows", offset=H + 4 * T, align_bytes=64)
         nc.gpsimd.memset(wc_scale_rows[:].bitcast(I32), 0)
         for q in range(4):
             nc.sync.dma_start(
@@ -181,7 +184,12 @@ def tile_list_ferry_charging_scores_kernel(
                 nc.vector.tensor_copy(out=out, in_=bank[:])
 
         def score_bank(tag):
-            return psum.tile([P, BANK], F32, name=tag, bufs=2 if tag == "bank1" else 3)
+            return psum.tile([P, BANK], F32, name=tag, bufs={"bank1": 2, "bank2": 3, "score": 3}[tag])
+
+        def last_pass(t, half):
+            if t == 0 and half == 1:
+                return [whole]
+            return [whole]
 
         def e_scores(t, half, tag):
             rows = slice(t * P, (t + 1) * P)
@@ -191,16 +199,18 @@ def tile_list_ferry_charging_scores_kernel(
                 if cols.start <= lo < cols.stop:
                     part = bank[:, lo - cols.start : hi - cols.start]
                     mm(part, wbq, rows, v_cols(lo, hi), slice(0, hi - lo), lo == cols.start, False)
-            for a in range(2):
-                mm(bank[:], waq[a], rows, hq[a, half], whole, False, a == 1)
+            mm(bank[:], waq[0], rows, hq[0, half], whole, False, False)
+            for part in last_pass(t, half):
+                mm(bank[:, part], waq[1], rows, hq[1, half], part, False, part.stop == BANK)
             empty("scalar", e_rows[t][:, cols], bank)
 
         def d_scores(t, half, tag, engine):
             rows = slice(t * P, (t + 1) * P)
             cols = slice(half * BANK, (half + 1) * BANK)
             bank = score_bank(tag)
-            for a in range(2):
-                mm(bank[:], (wc_codes[:, a, :], wc_plane), rows, hq[a, half], whole, a == 0, a == 1, lhs_row=4 * a)
+            mm(bank[:], (wc_codes[:, 0, :], wc_plane), rows, hq[0, half], whole, True, False)
+            for part in last_pass(t, half):
+                mm(bank[:, part], (wc_codes[:, 1, :], wc_plane), rows, hq[1, half], part, False, part.stop == BANK, lhs_row=4)
             empty(engine, d_rows[t][:, cols], bank)
 
         def h_half(b, half, w1q):
@@ -211,7 +221,13 @@ def tile_list_ferry_charging_scores_kernel(
 
         wc_plane = held([P, N], U8, "wc_plane")
 
+        wc_codes = held([P, 2, N], U32, "wc_codes")
+
         def deal_wc_plane():
+            nc.vector.tensor_copy(
+                out=wc_codes[:].rearrange("p a (t m) -> p a m t", t=PACK),
+                in_=wc_raw[:].bitcast(U32).rearrange("p a (m t) -> p a m t", t=PACK),
+            )
             nc.vector.tensor_copy(
                 out=wc_plane[:].rearrange("p (t m) -> p t m", t=PACK),
                 in_=wc_scale_rows[:].rearrange("p (m t) -> p t m", t=PACK),
@@ -221,17 +237,17 @@ def tile_list_ferry_charging_scores_kernel(
         w1q1 = quantize(w1r1, "w1q1")
         r00 = h_half(0, 0, w1q0)
         wbr = round_weight("scalar", wb_raw)
-        slot_tile = held([P, PACK, M], F32, "slot_tile", tag="w1_first")
+        slot_tile = reused.tile([P, PACK, M], F32, name="slot_tile", offset=4 * H, align_bytes=64)
         slot_t = load_rows(slot_tile[:], slot)
         r01 = h_half(0, 1, w1q0)
-        war0 = round_weight("scalar", wa_raw0)
+        war0 = round_weight("both", wa_raw0)
         hq[0, 0] = quantize(r00, "hq00")
         wbq = quantize(wbr, "wbq")
         r10 = h_half(1, 0, w1q1)
-        war1 = round_weight("vector", wa_raw1)
+        war1 = round_weight("both", wa_raw1)
         hq[1, 0] = quantize(r10, "hq10")
         deal_wc_plane()
-        row_values = reused.tile([P, 3, 8], F32, name="row_values", offset=0, align_bytes=64)
+        row_values = reused.tile([P, 3, 8], F32, name="row_values", offset=H + 4 * T, align_bytes=64)
         for k, vec in enumerate((scale, thresh, gain)):
             nc.sync.dma_start(row_values[:, k, 0:PACK], vec.rearrange("(p t) -> p t", t=PACK))
         row_scale, row_thresh, row_gain = (row_values[:, k, :] for k in range(3))
@@ -239,7 +255,7 @@ def tile_list_ferry_charging_scores_kernel(
         waq[1] = quantize(war1, "waq1")
         hq[0, 1] = quantize(r01, "hq01")
         r11 = h_half(1, 1, w1q1)
-        hq[1, 1] = quantize(r11, "hq11")
+        hq[1, 1] = quantize(r11, "hq11", ())
 
 
         HALF = M // 2
@@ -284,11 +300,11 @@ def tile_list_ferry_charging_scores_kernel(
             nc.sync.dma_start(out_1[0].rearrange("p m t -> p (m t)").bitcast(I32)[:, cols], y_codes[:, cols])
 
         for t in range(PACK):
-            e_scores(t, 0, "score")
             d_scores(t, 0, "score", "scalar")
-            e_scores(t, 1, "bank2")
+        for t in range(PACK):
+            e_scores(t, 0, "score")
             d_scores(t, 1, "bank1", "vector" if t == 0 else "scalar")
-
+            e_scores(t, 1, "bank2")
             if t < PACK - 1:
                 finish(t, 0, M)
         finish(PACK - 1, 0, HALF)

@@ -33,7 +33,7 @@ def tile_list_ferry_charging_scores_kernel(
         reused = ctx.enter_context(tc.tile_pool(name="reused", bufs=1))
         weights = ctx.enter_context(tc.tile_pool(name="weights", bufs=1))
         ring = ctx.enter_context(tc.tile_pool(name="ring", bufs=2))
-        deep = ctx.enter_context(tc.tile_pool(name="deep", bufs=16))
+        deep = ctx.enter_context(tc.tile_pool(name="deep", bufs=8))
         psum = ctx.enter_context(tc.psum_pool(name="psum", bufs=1))
 
         def held(shape, dtype, name, tag=None):
@@ -70,11 +70,11 @@ def tile_list_ferry_charging_scores_kernel(
             out = rounded[:].rearrange("p (t m j) -> p m j t", t=PACK, j=PACK)
             src = raw.rearrange("p j (m t) -> p m j t", t=PACK)
             if engine == "scalar":
-                for lo in range(0, P, P // 2):
-                    nc.scalar.copy(out=out[:, lo : lo + P // 2], in_=src[:, lo : lo + P // 2])
+                for lo in (0, 2):
+                    nc.scalar.copy(out=out[:, :, :, lo : lo + 2], in_=src[:, :, :, lo : lo + 2])
             elif engine == "both":
-                nc.scalar.copy(out=out[:, 0 : P // 2], in_=src[:, 0 : P // 2])
-                nc.vector.tensor_copy(out=out[:, P // 2 : P], in_=src[:, P // 2 : P])
+                nc.scalar.copy(out=out[:, :, :, 0:2], in_=src[:, :, :, 0:2])
+                nc.vector.tensor_copy(out=out[:, :, :, 2:4], in_=src[:, :, :, 2:4])
             elif engine == "gpsimd":
                 for lo in range(0, P, P // 4):
                     nc.gpsimd.tensor_scalar(
@@ -132,10 +132,13 @@ def tile_list_ferry_charging_scores_kernel(
         w1q0 = quantize(w1r0, "w1q0")
         v_pieces = []
         for lo, hi in ((0, 256), (256, 512), (512, 1024)):
-            piece = held([P, hi - lo], U32, "v_codes%d" % lo)
+            if lo < BANK:
+                piece = held([P, hi - lo], U32, "v_codes%d" % lo)
+            else:
+                piece = reused.tile([P, hi - lo], U32, name="v_codes%d" % lo, offset=H + 4 * T, align_bytes=64)
             nc.vector.tensor_copy(out=piece[:], in_=tab[:].bitcast(U32).indirect(offs_t[:, lo // 16 : hi // 16]))
             v_pieces.append((lo, hi, piece))
-            if lo == 0:
+            if hi == BANK:
                 nc.vector.tensor_copy(
                     out=w2_plane[:].rearrange("p (b t m) -> p b t m", b=2, t=PACK),
                     in_=w2_scale_rows[:].rearrange("p (b m t) -> p b t m", b=2, t=PACK),
@@ -145,7 +148,7 @@ def tile_list_ferry_charging_scores_kernel(
             first, piece = [(a, x) for a, b, x in v_pieces if a <= lo and hi <= b][0]
             return piece[:, lo - first : hi - first], v_plane[:, lo:hi]
 
-        wc_scale_rows = reused.tile([P, N], U8, name="wc_scale_rows", offset=H + 4 * T, align_bytes=64)
+        wc_scale_rows = reused.tile([P, N], U8, name="wc_scale_rows", offset=0, align_bytes=64)
         nc.gpsimd.memset(wc_scale_rows[:].bitcast(I32), 0)
         for q in range(4):
             nc.sync.dma_start(
@@ -153,23 +156,27 @@ def tile_list_ferry_charging_scores_kernel(
             )
         w2 = (w2_codes, w2_plane)
 
-        def w1_reading(w1q, c):
-            bank = psum.tile([P, PACK, CHUNK], F32, name="bank2", bufs=3)
-            for t in range(PACK):
-                mm(bank[:, t, :], w1q, slice(t * P, (t + 1) * P), v_cols(c * CHUNK, (c + 1) * CHUNK), slice(0, CHUNK), True, True)
-            h1 = deep.tile([P, CHUNK, PACK], F32, name="h1")
-            nc.scalar.copy(out=h1[:], in_=bank[:].rearrange("p t n -> p n t"))
+        def w1_reading(w1q, pair):
+            cols = v_cols(2 * pair * CHUNK, 2 * (pair + 1) * CHUNK)
+            h1 = deep.tile([P, 2, 2 * CHUNK, 2], F32, name="h1")
+            for u in range(2):
+                bank = psum.tile([P, 2, 2 * CHUNK], F32, name="bank2", bufs=3)
+                for s in range(2):
+                    t = 2 * u + s
+                    mm(bank[:, s, :], w1q, slice(t * P, (t + 1) * P), cols, slice(0, 2 * CHUNK), True, True)
+                nc.scalar.copy(out=h1[:, u], in_=bank[:].rearrange("p s n -> p n s"))
             return h1
 
         def lesser(b, c, h1, h_rounded):
-            bank = psum.tile([P, PACK, CHUNK], F32, name="bank1", bufs=2)
+            bank = psum.tile([P, PACK, CHUNK], F32, name="bank1", bufs=3)
             for t in range(PACK):
                 lo = b * PASS + t * P
                 mm(bank[:, t, :], w2, slice(lo, lo + P), v_cols(c * CHUNK, (c + 1) * CHUNK), slice(0, CHUNK), True, True, FP4X4)
             lo = (c % PACK) * BANK
             nc.vector.tensor_tensor(
-                out=h_rounded[:, lo : lo + BANK].rearrange("p (n t) -> p n t", t=PACK),
-                in0=bank[:].rearrange("p t n -> p n t"), in1=h1[:], op=ALU.min,
+                out=h_rounded[:, lo : lo + BANK].rearrange("p (n u s) -> p n u s", u=2, s=2),
+                in0=bank[:].rearrange("p (u s) n -> p n u s", u=2),
+                in1=h1[:, :, (c % 2) * CHUNK : (c % 2 + 1) * CHUNK, :].rearrange("p u n s -> p n u s"), op=ALU.min,
             )
 
         e_rows = [held([P, S], F32, "e_rows%d" % t) for t in range(PACK)]
@@ -184,7 +191,7 @@ def tile_list_ferry_charging_scores_kernel(
                 nc.vector.tensor_copy(out=out, in_=bank[:])
 
         def score_bank(tag):
-            return psum.tile([P, BANK], F32, name=tag, bufs={"bank1": 2, "bank2": 3, "score": 3}[tag])
+            return psum.tile([P, BANK], F32, name=tag, bufs={"bank1": 3, "bank2": 3, "score": 2}[tag])
 
         def last_pass(t, half):
             if t == 0 and half == 1:
@@ -215,8 +222,10 @@ def tile_list_ferry_charging_scores_kernel(
 
         def h_half(b, half, w1q):
             h_rounded = ring.tile([P, PACK * BANK], BF16, name="h_rounded", align_bytes=64)
-            for c in range(PACK * half, PACK * (half + 1)):
-                lesser(b, c, w1_reading(w1q, c), h_rounded)
+            for pair in range(2 * half, 2 * (half + 1)):
+                h1 = w1_reading(w1q, pair)
+                for c in (2 * pair, 2 * pair + 1):
+                    lesser(b, c, h1, h_rounded)
             return h_rounded
 
         wc_plane = held([P, N], U8, "wc_plane")
@@ -247,7 +256,7 @@ def tile_list_ferry_charging_scores_kernel(
         war1 = round_weight("both", wa_raw1)
         hq[1, 0] = quantize(r10, "hq10")
         deal_wc_plane()
-        row_values = reused.tile([P, 3, 8], F32, name="row_values", offset=H + 4 * T, align_bytes=64)
+        row_values = reused.tile([P, 3, 8], F32, name="row_values", offset=0, align_bytes=64)
         for k, vec in enumerate((scale, thresh, gain)):
             nc.sync.dma_start(row_values[:, k, 0:PACK], vec.rearrange("(p t) -> p t", t=PACK))
         row_scale, row_thresh, row_gain = (row_values[:, k, :] for k in range(3))
@@ -300,9 +309,8 @@ def tile_list_ferry_charging_scores_kernel(
             nc.sync.dma_start(out_1[0].rearrange("p m t -> p (m t)").bitcast(I32)[:, cols], y_codes[:, cols])
 
         for t in range(PACK):
-            d_scores(t, 0, "score", "scalar")
-        for t in range(PACK):
             e_scores(t, 0, "score")
+            d_scores(t, 0, "score", "scalar")
             d_scores(t, 1, "bank1", "vector" if t == 0 else "scalar")
             e_scores(t, 1, "bank2")
             if t < PACK - 1:

from contextlib import ExitStack

import concourse.mybir as mybir

K, T, H, N, S, M = 512, 4096, 1024, 512, 1024, 512
FLOPS = 2 * (2 * K * H * S + H * N * S + K * N * S + H * N * S)

F32 = mybir.dt.float32
BF16 = mybir.dt.bfloat16
I32 = mybir.dt.int32
U32 = mybir.dt.uint32
U16 = mybir.dt.uint16
U8 = mybir.dt.uint8
FP8X4 = mybir.dt.float8_e4m3fn_x4
FP4X4 = mybir.dt.float4_e2m1fn_x4
ALU = mybir.AluOpType
ACT = mybir.ActivationFunctionType

P = 128
PACK = 4
PASS = P * PACK
BANK = 512
CHUNK = BANK // PACK


def tile_list_ferry_charging_scores_kernel(
    tc, tab_words, tab_scales, offs, pos1, pos2, w1, w2_words, w2_scales, wa, wb,
    wc_words, wc_scales, scale, thresh, slot, gain, out_0, out_1, out_2,
):
    nc = tc.nc
    with ExitStack() as ctx:
        keep = ctx.enter_context(tc.tile_pool(name="keep", bufs=1))
        reused = ctx.enter_context(tc.tile_pool(name="reused", bufs=1))
        weights = ctx.enter_context(tc.tile_pool(name="weights", bufs=1))
        ring = ctx.enter_context(tc.tile_pool(name="ring", bufs=2))
        deep = ctx.enter_context(tc.tile_pool(name="deep", bufs=8))
        psum = ctx.enter_context(tc.psum_pool(name="psum", bufs=1))

        def held(shape, dtype, name, tag=None):
            return keep.tile(shape, dtype, name=name, tag=tag or name, align_bytes=64)

        tab_scale_rows = held([P, T], U8, "tab_scale_rows")
        nc.vector.memset(tab_scale_rows[:].bitcast(I32), 0)

        w2_raw = [
            reused.tile([P, PASS], U16, name="w2_raw%d" % b, offset=b * (H + 4 * T), align_bytes=64) for b in range(2)
        ]
        offs_t = keep.tile([P, S // 16], U16, name="offs_t")
        pos1_t = keep.tile([P, M // 16], U16, name="pos1_t")
        pos2_t = keep.tile([P, M // 16], U16, name="pos2_t")
        for b in range(2):
            nc.sync.dma_start(w2_raw[b][:].bitcast(I32), w2_words[0, :, b * H : (b + 1) * H].bitcast(I32))
        nc.sync.dma_start(offs_t[:], offs)
        nc.sync.dma_start(pos1_t[:], pos1)
        nc.sync.dma_start(pos2_t[:], pos2)

        def load_rows(raw, rows):
            nc.sync.dma_start(raw, rows.rearrange("(p j) c -> p j c", j=PACK))
            return raw

        w1_first = weights.tile([P, PACK, N], F32, name="w1_first", offset=0, align_bytes=64)
        w1_raw0 = load_rows(w1_first[:], w1[:, 0:PASS])
        for q in range(4):
            nc.sync.dma_start(
                tab_scale_rows[32 * q : 32 * q + 4, :].bitcast(I32), tab_scales[0, 4 * q : 4 * q + 4, :].bitcast(I32)
            )

        def round_weight(engine, raw):
            rounded = ring.tile([P, PACK * N], BF16, name="rounded", align_bytes=64, bufs=3)
            out = rounded[:].rearrange("p (t m j) -> p m j t", t=PACK, j=PACK)
            src = raw.rearrange("p j (m t) -> p m j t", t=PACK)
            if engine == "scalar":
                for lo in (0, 2):
                    nc.scalar.copy(out=out[:, :, :, lo : lo + 2], in_=src[:, :, :, lo : lo + 2])
            elif engine == "both":
                nc.scalar.copy(out=out[:, :, :, 0:2], in_=src[:, :, :, 0:2])
                nc.vector.tensor_copy(out=out[:, :, :, 2:4], in_=src[:, :, :, 2:4])
            elif engine == "gpsimd":
                for lo in range(0, P, P // 4):
                    nc.gpsimd.tensor_scalar(
                        out=out[:, lo : lo + P // 4], in0=src[:, lo : lo + P // 4], scalar1=1.0, scalar2=0.0,
                        op0=ALU.mult, op1=ALU.add,
                    )
            else:
                nc.vector.tensor_copy(out=out, in_=src)
            return rounded

        def quantize(rounded, name, cuts=()):
            width = rounded.shape[1] // PACK
            codes = held([P, width], U32, name + "_codes")
            scales = held([P, width], U8, name + "_scales")
            edges = (0, *cuts, width)
            for lo, hi in zip(edges, edges[1:]):
                nc.vector.quantize_mx(
                    out=codes[:, lo:hi].bitcast(FP8X4), scales=scales[:, lo:hi], in_=rounded[:, PACK * lo : PACK * hi]
                )
            return codes, scales

        def mm(out, lhs, lhs_cols, rhs, rhs_cols, start, stop, lhs_dtype=FP8X4, lhs_row=0):
            nc.tensor.matmul_mx(
                out=out,
                lhsT=lhs[0][:, lhs_cols].bitcast(lhs_dtype), lhsT_scale=lhs[1][lhs_row:P, lhs_cols],
                rhs=rhs[0][:, rhs_cols].bitcast(FP8X4), rhs_scale=rhs[1][:, rhs_cols],
                start=start, stop=stop,
            )

        w2_codes = held([P, H], U16, "w2_codes")
        w2_plane = held([P, H], U8, "w2_plane")
        for b in range(2):
            nc.vector.tensor_copy(
                out=w2_codes[:, b * PASS : (b + 1) * PASS].rearrange("p (t m) -> p t m", t=PACK),
                in_=w2_raw[b][:].rearrange("p (m t) -> p t m", t=PACK),
            )
        tab = reused.tile([P, T], I32, name="tab", offset=0, align_bytes=64)
        nc.sync.dma_start(tab[:], tab_words[0].rearrange("p t i -> p (t i)").bitcast(I32))
        w2_scale_rows = reused.tile([P, H], U8, name="w2_scale_rows", offset=H + 4 * T, align_bytes=64)
        nc.vector.memset(w2_scale_rows[:].bitcast(I32), 0)
        for q in range(4):
            nc.sync.dma_start(
                w2_scale_rows[32 * q : 32 * q + 4, :].bitcast(I32), w2_scales[0, 4 * q : 4 * q + 4, :].bitcast(I32)
            )
        v_plane = held([P, S], U8, "v_plane")
        nc.vector.tensor_copy(out=v_plane[:], in_=tab_scale_rows[:].indirect(offs_t[:]))
        w1r0 = round_weight("scalar", w1_raw0)
        early = weights.tile([P, 4, PACK, N], F32, name="early", offset=4 * H, align_bytes=64)
        w1_raw1 = load_rows(early[:, 0], w1[:, PASS : 2 * PASS])
        wc_raw = weights.tile([P, 2, N], I32, name="wc_raw", offset=0, align_bytes=64)
        nc.sync.dma_start(wc_raw[:], wc_words.rearrange("a p c i -> p a (c i)").bitcast(I32))
        wb_raw = load_rows(early[:, 1], wb)
        wa_raw0 = load_rows(early[:, 2], wa[0:PASS, :])
        wa_raw1 = load_rows(early[:, 3], wa[PASS : 2 * PASS, :])
        w1q0 = quantize(w1r0, "w1q0")
        v_pieces = []
        for lo, hi in ((0, 256), (256, 512), (512, 1024)):
            if lo < BANK:
                piece = held([P, hi - lo], U32, "v_codes%d" % lo)
            else:
                piece = reused.tile([P, hi - lo], U32, name="v_codes%d" % lo, offset=H + 4 * T, align_bytes=64)
            nc.vector.tensor_copy(out=piece[:], in_=tab[:].bitcast(U32).indirect(offs_t[:, lo // 16 : hi // 16]))
            v_pieces.append((lo, hi, piece))
            if hi == BANK:
                nc.vector.tensor_copy(
                    out=w2_plane[:].rearrange("p (b t m) -> p b t m", b=2, t=PACK),
                    in_=w2_scale_rows[:].rearrange("p (b m t) -> p b t m", b=2, t=PACK),
                )

        def v_cols(lo, hi):
            first, piece = [(a, x) for a, b, x in v_pieces if a <= lo and hi <= b][0]
            return piece[:, lo - first : hi - first], v_plane[:, lo:hi]

        wc_scale_rows = reused.tile([P, N], U8, name="wc_scale_rows", offset=0, align_bytes=64)
        nc.gpsimd.memset(wc_scale_rows[:].bitcast(I32), 0)
        for q in range(4):
            nc.sync.dma_start(
                wc_scale_rows[32 * q : 32 * q + 8, :].bitcast(I32), wc_scales[:, 4 * q : 4 * q + 4, :].bitcast(I32)
            )
        w2 = (w2_codes, w2_plane)

        def w1_reading(w1q, pair):
            cols = v_cols(2 * pair * CHUNK, 2 * (pair + 1) * CHUNK)
            h1 = deep.tile([P, 2, 2 * CHUNK, 2], F32, name="h1")
            for u in range(2):
                bank = psum.tile([P, 2, 2 * CHUNK], F32, name="bank2", bufs=3)
                for s in range(2):
                    t = 2 * u + s
                    mm(bank[:, s, :], w1q, slice(t * P, (t + 1) * P), cols, slice(0, 2 * CHUNK), True, True)
                nc.scalar.copy(out=h1[:, u], in_=bank[:].rearrange("p s n -> p n s"))
            return h1

        def lesser(b, c, h1, h_rounded):
            bank = psum.tile([P, PACK, CHUNK], F32, name="bank1", bufs=3)
            for t in range(PACK):
                lo = b * PASS + t * P
                mm(bank[:, t, :], w2, slice(lo, lo + P), v_cols(c * CHUNK, (c + 1) * CHUNK), slice(0, CHUNK), True, True, FP4X4)
            lo = (c % PACK) * BANK
            nc.vector.tensor_tensor(
                out=h_rounded[:, lo : lo + BANK].rearrange("p (n u s) -> p n u s", u=2, s=2),
                in0=bank[:].rearrange("p (u s) n -> p n u s", u=2),
                in1=h1[:, :, (c % 2) * CHUNK : (c % 2 + 1) * CHUNK, :].rearrange("p u n s -> p n u s"), op=ALU.min,
            )

        e_rows = [held([P, S], F32, "e_rows%d" % t) for t in range(PACK)]
        d_rows = [held([P, S], F32, "d_rows%d" % t) for t in range(PACK)]
        whole = slice(0, BANK)
        hq, waq = {}, {}

        def empty(engine, out, bank):
            if engine == "scalar":
                nc.scalar.copy(out=out, in_=bank[:])
            else:
                nc.vector.tensor_copy(out=out, in_=bank[:])

        def score_bank(tag):
            return psum.tile([P, BANK], F32, name=tag, bufs={"bank1": 3, "bank2": 3, "score": 2}[tag])

        def last_pass(t, half):
            if t == 0 and half == 1:
                return [whole]
            return [whole]

        def e_scores(t, half, tag):
            rows = slice(t * P, (t + 1) * P)
            cols = slice(half * BANK, (half + 1) * BANK)
            bank = score_bank(tag)
            for lo, hi, piece in v_pieces:
                if cols.start <= lo < cols.stop:
                    part = bank[:, lo - cols.start : hi - cols.start]
                    mm(part, wbq, rows, v_cols(lo, hi), slice(0, hi - lo), lo == cols.start, False)
            mm(bank[:], waq[0], rows, hq[0, half], whole, False, False)
            for part in last_pass(t, half):
                mm(bank[:, part], waq[1], rows, hq[1, half], part, False, part.stop == BANK)
            empty("scalar", e_rows[t][:, cols], bank)

        def d_scores(t, half, tag, engine):
            rows = slice(t * P, (t + 1) * P)
            cols = slice(half * BANK, (half + 1) * BANK)
            bank = score_bank(tag)
            mm(bank[:], (wc_codes[:, 0, :], wc_plane), rows, hq[0, half], whole, True, False)
            for part in last_pass(t, half):
                mm(bank[:, part], (wc_codes[:, 1, :], wc_plane), rows, hq[1, half], part, False, part.stop == BANK, lhs_row=4)
            empty(engine, d_rows[t][:, cols], bank)

        def h_half(b, half, w1q):
            h_rounded = ring.tile([P, PACK * BANK], BF16, name="h_rounded", align_bytes=64)
            for pair in range(2 * half, 2 * (half + 1)):
                h1 = w1_reading(w1q, pair)
                for c in (2 * pair, 2 * pair + 1):
                    lesser(b, c, h1, h_rounded)
            return h_rounded

        wc_plane = held([P, N], U8, "wc_plane")

        wc_codes = held([P, 2, N], U32, "wc_codes")

        def deal_wc_plane():
            nc.vector.tensor_copy(
                out=wc_codes[:].rearrange("p a (t m) -> p a m t", t=PACK),
                in_=wc_raw[:].bitcast(U32).rearrange("p a (m t) -> p a m t", t=PACK),
            )
            nc.vector.tensor_copy(
                out=wc_plane[:].rearrange("p (t m) -> p t m", t=PACK),
                in_=wc_scale_rows[:].rearrange("p (m t) -> p t m", t=PACK),
            )

        w1r1 = round_weight("both", w1_raw1)
        w1q1 = quantize(w1r1, "w1q1")
        r00 = h_half(0, 0, w1q0)
        wbr = round_weight("scalar", wb_raw)
        slot_tile = reused.tile([P, PACK, M], F32, name="slot_tile", offset=4 * H, align_bytes=64)
        slot_t = load_rows(slot_tile[:], slot)
        r01 = h_half(0, 1, w1q0)
        war0 = round_weight("both", wa_raw0)
        hq[0, 0] = quantize(r00, "hq00")
        wbq = quantize(wbr, "wbq")
        r10 = h_half(1, 0, w1q1)
        war1 = round_weight("both", wa_raw1)
        hq[1, 0] = quantize(r10, "hq10")
        deal_wc_plane()
        row_values = reused.tile([P, 3, 8], F32, name="row_values", offset=0, align_bytes=64)
        for k, vec in enumerate((scale, thresh, gain)):
            nc.sync.dma_start(row_values[:, k, 0:PACK], vec.rearrange("(p t) -> p t", t=PACK))
        row_scale, row_thresh, row_gain = (row_values[:, k, :] for k in range(3))
        waq[0] = quantize(war0, "waq0")
        waq[1] = quantize(war1, "waq1")
        hq[0, 1] = quantize(r01, "hq01")
        r11 = h_half(1, 1, w1q1)
        hq[1, 1] = quantize(r11, "hq11", ())


        HALF = M // 2
        y = held([P, 2, PACK, HALF], F32, "y")
        y_rounded = held([P, PACK * M], BF16, "y_rounded")
        y_codes = held([P, M], I32, "y_codes")
        y_plane = held([P, M], U8, "y_plane")
        out_rows = out_0.rearrange("(p t) (h m) -> p h t m", t=PACK, h=2)

        def finish(t, lo, hi):
            width = hi - lo
            halves = slice(lo // HALF, hi // HALF)
            gate = ring.tile([P, width], F32, name="gate")
            nc.scalar.activation(
                out=gate[:], in_=e_rows[t][:].indirect(pos1_t[:, lo // 16 : hi // 16]), func=ACT.Sigmoid,
                bias=row_thresh[:, t : t + 1], scale=row_scale[:, t : t + 1],
            )
            weighted = ring.tile([P, width], F32, name="weighted")
            nc.vector.tensor_tensor(
                out=weighted[:], in0=d_rows[t][:].indirect(pos2_t[:, lo // 16 : hi // 16]), in1=slot_t[:, t, lo:hi],
                op=ALU.mult,
            )
            total = ring.tile([P, width], F32, name="total")
            nc.vector.tensor_tensor(out=total[:], in0=weighted[:], in1=gate[:], op=ALU.add)
            nc.vector.scalar_tensor_tensor(
                out=y[:, halves, t, :], in0=total[:].rearrange("p (h m) -> p h m", m=HALF),
                scalar=row_gain[:, t : t + 1], in1=gate[:].rearrange("p (h m) -> p h m", m=HALF),
                op0=ALU.mult, op1=ALU.mult,
            )
            nc.sync.dma_start(out_rows[:, halves, t, :], y[:, halves, t, :])

        def planes(engine, h):
            cols = slice(h * HALF, (h + 1) * HALF)
            rounded = y_rounded[:, h * HALF * PACK : (h + 1) * HALF * PACK]
            out = rounded.rearrange("p (c i t) -> p c t i", i=PACK, t=PACK)
            src = y[:, h, :, :].rearrange("p t (c i) -> p c t i", i=PACK)
            if engine == "scalar":
                nc.scalar.copy(out=out, in_=src)
            else:
                nc.vector.tensor_copy(out=out, in_=src)
            nc.vector.quantize_mx(out=y_codes[:, cols].bitcast(FP8X4), scales=y_plane[:, cols], in_=rounded)
            nc.sync.dma_start(out_1[0].rearrange("p m t -> p (m t)").bitcast(I32)[:, cols], y_codes[:, cols])

        for t in range(PACK):
            e_scores(t, 0, "score")
            d_scores(t, 0, "score", "scalar")
            d_scores(t, 1, "bank1", "vector" if t == 0 else "scalar")
            e_scores(t, 1, "bank2")
            if t < PACK - 1:
                finish(t, 0, M)
        finish(PACK - 1, 0, HALF)
        finish(PACK - 1, HALF, M)
        planes("scalar", 0)
        planes("vector", 1)

        for q in range(4):
            queue = nc.scalar if q % 2 else nc.sync
            queue.dma_start(
                out_2[0, 4 * q : 4 * q + 4, :].bitcast(I32), y_plane[32 * q : 32 * q + 4, :].bitcast(I32)
            )
